import numpy as np
import ml_dtypes


def mxq(x, axis, fmt="e4m3"):
    dtype, down = {"e4m3": (ml_dtypes.float8_e4m3fn, 7), "e5m2": (ml_dtypes.float8_e5m2, 14)}[fmt]
    v = np.moveaxis(np.asarray(x, np.float32).astype(ml_dtypes.bfloat16).astype(np.float64), axis, -1)
    blocks = v.reshape(v.shape[:-1] + (-1, 32))
    amax = np.abs(blocks).max(-1, keepdims=True)
    byte = np.maximum(np.where(amax > 0, np.frexp(amax)[1] - 1 + 127, 0) - down, 1)
    scale = np.exp2(byte - 127.0)
    codes = (blocks / scale).astype(np.float32).astype(dtype).astype(np.float64)
    return np.moveaxis((codes * scale).reshape(v.shape), -1, axis)


WIDE = False


def mx_kscale(k):
    if not WIDE:
        return np.ones(k)
    levels = np.array([10, -10, 5, -5, 0])
    if k % 512:
        return np.exp2(np.random.permutation(np.resize(levels, k // 32))).repeat(32)
    a = np.empty((k // 512, 16))
    for p in range(k // 512):
        a[p, :8] = np.random.permutation(np.resize(levels, 8))
        for g in range(8):
            far = levels[np.abs(levels - a[p, g]) >= 10]
            a[p, g + 8] = far[np.random.randint(len(far))]
    return np.exp2(a.ravel()).repeat(32)


def f64(x):
    return np.asarray(x).astype(np.float64)


def striped(idx):
    return np.tile(idx.reshape(-1, 16).T, (8, 1)).astype(np.uint16)


def unstriped(offs):
    return offs[:16].T.reshape(-1).astype(np.int64)


def striped8(idx):
    return np.concatenate([x.reshape(-1, 16).T for x in idx]).astype(np.uint16)


def runs(offs, k):
    lists = np.stack([offs[16 * r : 16 * r + 16].T.reshape(-1) for r in range(8)]).astype(np.int64)
    return lists[np.arange(k) % 512 // 64]


def pack_weight(w):
    k, n = w.shape
    w = f64(np.asarray(w, np.float32).astype(ml_dtypes.bfloat16)).reshape(k // 32, 32, n)
    amax = np.abs(w).max(1)
    byte = np.clip(np.where(amax > 0, np.frexp(amax)[1] - 1 + 127 - 7, 1), 1, 254)
    scaled = (w * np.exp2(127.0 - byte)[:, None, :]).reshape(k, n).astype(np.float32)
    words = np.ascontiguousarray(scaled.reshape(k // 512, 128, 4, n).transpose(0, 1, 3, 2)).astype(ml_dtypes.float8_e4m3fn).view(np.uint8)
    return words, np.ascontiguousarray(byte.astype(np.uint8).reshape(k // 512, 16, n))


def unpack_weight(words, scales):
    g, p, n, _ = words.shape
    vals = np.ascontiguousarray(words).view(ml_dtypes.float8_e4m3fn).astype(np.float64) * np.repeat(np.exp2(scales.astype(np.float64) - 127.0), 8, axis=1)[..., None]
    return vals.transpose(0, 1, 3, 2).reshape(g * 512, n)


K, T, S, H, G, W = 512, 1024, 512, 512, 2048, 256


def setup_inputs():
    n = np.random.standard_normal
    s = mx_kscale(K)[:, None]
    packed_xT = pack_weight(n((K, T)) * s)
    packed_dT = pack_weight(n((K, G)) / s)
    perm = np.stack([np.random.permutation(S) for _ in range(8)])
    return {
        "x_words": packed_xT[0],
        "x_scales": packed_xT[1],
        "w1": (n((K, H)) / np.sqrt(K) / s).astype(np.float32),
        "w2": (n((K, H)) / np.sqrt(K) / s).astype(np.float32),
        "gs": (np.random.uniform(0.5, 1.5, (K, 1)) * s).astype(np.float32),
        "d_words": packed_dT[0],
        "d_scales": packed_dT[1],
        "offs": striped(np.random.permutation(T)[:S]),
        "two": striped(np.random.permutation(T)[:S]),
        "n1": striped8(np.stack([np.random.permutation(S) for _ in range(8)])),
        "n2": striped8(np.stack([np.random.permutation(S) for _ in range(8)])),
        "k1": striped8(np.random.randint(0, G, (8, H))),
        "n3": striped8(perm[:, :W]),
        "n4": striped8(perm[:, W:]),
    }


def reference(x_words, x_scales, w1, w2, gs, d_words, d_scales, offs, two, n1, n2, k1, n3, n4):
    d_k1 = unpack_weight(d_words, d_scales)[np.arange(K)[:, None], runs(k1, K)]
    xq = unpack_weight(x_words, x_scales)[:, unstriped(offs)]
    y = mxq(f64(w1), 0, "e4m3").T @ xq
    x_two = unpack_weight(x_words, x_scales)[:, unstriped(two)]
    d = mxq(f64(w2), 0, "e4m3").T @ x_two
    z = f64(gs) * (y * (np.tanh(d[np.arange(H)[:, None], runs(n1, H)] - (d[np.arange(H)[:, None], runs(n2, H)]))))
    h = 0.0625 * ((d_k1.T @ mxq(z, 0, "e4m3")))
    pa = h[np.arange(H)[:, None], runs(n3, H)]
    pb = h[np.arange(H)[:, None], runs(n4, H)]
    ra = np.maximum(pa, pb)
    out = h.copy()
    out[np.arange(H)[:, None], runs(n3, H)] = ra
    return out

@@ -1,0 +1,183 @@
+from contextlib import ExitStack
+
+import concourse.mybir as mybir
+
+K, T, S, H, G, W = 512, 1024, 512, 512, 2048, 256
+P = 128
+PACK = 4
+FLOPS = 3 * 2 * K * H * S
+
+F32 = mybir.dt.float32
+BF16 = mybir.dt.bfloat16
+I32 = mybir.dt.int32
+U32 = mybir.dt.uint32
+U16 = mybir.dt.uint16
+U8 = mybir.dt.uint8
+FP8X4 = mybir.dt.float8_e4m3fn_x4
+ACT = mybir.ActivationFunctionType
+ALU = mybir.AluOpType
+
+CHUNKS = ((0, 256), (256, 128), (384, 128))
+W_PIECES = 2
+
+
+def tile_picked_twqjointbfill_none_p_kernel(
+    tc, x_words, x_scales, w1, w2, gs, d_words, d_scales, offs, two, n1, n2, k1, n3, n4, out
+):
+    nc = tc.nc
+    with ExitStack() as ctx:
+        lists = ctx.enter_context(tc.tile_pool(name="lists", bufs=1))
+        sb = ctx.enter_context(tc.tile_pool(name="sb", bufs=1))
+        psum = ctx.enter_context(tc.psum_pool(name="psum", bufs=1))
+
+        def load_list(name, src):
+            tile = lists.tile([P, src.shape[1]], U16, name=name)
+            nc.sync.dma_start(tile[:], src)
+            return tile
+
+        def entries(tile, start, count):
+            return tile[:, start // 16 : (start + count) // 16]
+
+        def load_weight(name, src):
+            pieces = []
+            width = H // W_PIECES
+            rows = src.rearrange("(p j) c -> p j c", j=PACK)
+            for a in range(W_PIECES):
+                raw = sb.tile([P, PACK, width], F32, name=f"{name}_raw{a}")
+                nc.sync.dma_start(raw[:], rows[:, :, a * width : (a + 1) * width])
+                pieces.append(raw)
+            return pieces
+
+        def quantise_weight(name, pieces):
+            grouped = sb.tile([P, PACK * H], BF16, name=f"{name}_bf", align_bytes=64)
+            codes = sb.tile([P, H], U32, name=f"{name}_codes", align_bytes=64)
+            scales = sb.tile([P, H], U8, name=f"{name}_scales", align_bytes=64)
+            dealt = grouped[:].rearrange("p (t m j) -> p m j t", t=PACK, j=PACK)
+            per = P // len(pieces)
+            for a, raw in enumerate(pieces):
+                nc.scalar.copy(out=dealt[:, a * per : (a + 1) * per], in_=raw[:].rearrange("p j (m t) -> p m j t", t=PACK))
+            for t in range(PACK):
+                cols = slice(t * P, (t + 1) * P)
+                nc.vector.quantize_mx(
+                    out=codes[:, cols].bitcast(FP8X4), scales=scales[:, cols], in_=grouped[:, t * PACK * P : (t + 1) * PACK * P]
+                )
+            return codes, scales
+
+        xw = sb.tile([P, T], I32, name="xw", align_bytes=64)
+        xs = sb.tile([P, T], U8, name="xs", align_bytes=64)
+        dw = sb.tile([P, G], I32, name="dw", align_bytes=64)
+        ds = sb.tile([P, G], U8, name="ds", align_bytes=64)
+        gain = sb.tile([P, PACK], F32, name="gain")
+
+        nc.gpsimd.memset(xs[:].bitcast(I32), 0)
+        nc.gpsimd.memset(ds[:].bitcast(I32), 0)
+        nc.sync.dma_start(xw[:], x_words[0].rearrange("p n t -> p (n t)").bitcast(I32))
+        two_l = load_list("two_l", two)
+        xs_rows = x_scales[0].bitcast(I32)
+        for j in range(4):
+            nc.sync.dma_start(xs[:].bitcast(I32)[j:P:32, :], xs_rows[j:16:4, :])
+        w2_raw = load_weight("w2", w2)
+        offs_l = load_list("offs_l", offs)
+        w1_raw = load_weight("w1", w1)
+        n2_l = load_list("n2_l", n2)
+        n1_l = load_list("n1_l", n1)
+        k1_l = load_list("k1_l", k1)
+        nc.sync.dma_start(dw[:], d_words[0].rearrange("p n t -> p (n t)").bitcast(I32))
+        n3_l = load_list("n3_l", n3)
+        n4_l = load_list("n4_l", n4)
+        ds_rows = d_scales[0].bitcast(I32)
+        for e in range(2):
+            nc.gpsimd.dma_start(ds[:].bitcast(I32)[e:P:16, :], ds_rows[e:16:2, :])
+        nc.gpsimd.dma_start(gain[:], gs.rearrange("(p t) o -> p (t o)", t=PACK))
+
+        def pick(name, words, scales, offsets):
+            codes = sb.tile([P, S], U32, name=f"{name}_codes", align_bytes=64)
+            plane = sb.tile([P, S], U8, name=f"{name}_plane", align_bytes=64)
+            nc.vector.tensor_copy(codes[:], words[:].bitcast(U32).indirect(offsets[:]))
+            nc.vector.tensor_copy(plane[:], scales[:].indirect(offsets[:]))
+            return codes, plane
+
+        def product(bank, stat, t, mov, cols):
+            tcols = slice(t * P, (t + 1) * P)
+            nc.tensor.matmul_mx(
+                out=bank[:, cols],
+                lhsT=stat[0][:, tcols].bitcast(FP8X4),
+                lhsT_scale=stat[1][:, tcols],
+                rhs=mov[0][:, cols].bitcast(FP8X4),
+                rhs_scale=mov[1][:, cols],
+                start=True,
+                stop=True,
+            )
+
+        everything = slice(0, S)
+        x_two = pick("x_two", xw, xs, two_l)
+        w2_q = quantise_weight("w2", w2_raw)
+        d_rows = []
+        for t in range(PACK):
+            bank = psum.tile([P, S], F32, name=f"d_bank{t}", tag=f"dh{t}")
+            product(bank, w2_q, t, x_two, everything)
+            row = sb.tile([P, S], F32, name=f"d_row{t}")
+            nc.scalar.copy(out=row[:], in_=bank[:])
+            d_rows.append(row)
+
+        x_idx = pick("x_idx", xw, xs, offs_l)
+        w1_q = quantise_weight("w1", w1_raw)
+        y_banks = []
+        for t in range(PACK):
+            bank = psum.tile([P, S], F32, name=f"y_bank{t}", tag=f"y{t}")
+            product(bank, w1_q, t, x_idx, everything)
+            y_banks.append(bank)
+
+        def dictionary():
+            codes, plane = pick("d_k1", dw, ds, k1_l)
+            codes_dealt = sb.tile([P, H], U32, name="dk_codes", align_bytes=64)
+            plane_dealt = sb.tile([P, H], U8, name="dk_plane", align_bytes=64)
+            nc.vector.tensor_copy(plane_dealt[:].rearrange("p (t m) -> p m t", t=PACK), plane[:].rearrange("p (m t) -> p m t", t=PACK))
+            rows = plane_dealt[:].bitcast(I32)
+            for e in range(2):
+                nc.sync.dma_start(rows[2 + e : P : 32, :], rows[16 + e : P : 32, :])
+            nc.vector.tensor_copy(codes_dealt[:].rearrange("p (t m) -> p m t", t=PACK), codes[:].rearrange("p (m t) -> p m t", t=PACK))
+            return codes_dealt, plane_dealt
+
+        z_codes = sb.tile([P, S], U32, name="z_codes", align_bytes=64)
+        z_scales = sb.tile([P, S], U8, name="z_scales", align_bytes=64)
+        h_banks = [psum.tile([P, S], F32, name=f"h_bank{t}", tag=f"dh{t}") for t in range(PACK)]
+        h_rows = [sb.tile([P, S], F32, name=f"h_row{t}") for t in range(PACK)]
+        dk_q = None
+        for c, (start, width) in enumerate(CHUNKS):
+            cols = slice(start, start + width)
+            z_planes = sb.tile([P, PACK, width], BF16, name=f"z_planes{c}")
+            for t in range(PACK):
+                second = sb.tile([P, width], F32, name=f"second{c}_{t}")
+                diff = sb.tile([P, width], F32, name=f"diff{c}_{t}")
+                bent = sb.tile([P, width], F32, name=f"bent{c}_{t}")
+                nc.scalar.activation(out=second[:], in_=d_rows[t][:].indirect(entries(n2_l, start, width)), func=ACT.Copy)
+                nc.vector.tensor_tensor(diff[:], d_rows[t][:].indirect(entries(n1_l, start, width)), second[:], ALU.subtract)
+                nc.scalar.activation(out=bent[:], in_=diff[:], func=ACT.Tanh)
+                nc.vector.scalar_tensor_tensor(
+                    out=z_planes[:, t, :], in0=y_banks[t][:, cols], scalar=gain[:, t : t + 1], in1=bent[:], op0=ALU.mult, op1=ALU.mult
+                )
+            if c == 0:
+                dk_q = dictionary()
+            z_woven = sb.tile([P, PACK * width], BF16, name=f"z_woven{c}", align_bytes=64)
+            nc.vector.tensor_copy(
+                z_woven[:].rearrange("p (c i t) -> p c t i", i=4, t=PACK), z_planes[:].rearrange("p t (c i) -> p c t i", i=4)
+            )
+            nc.vector.quantize_mx(out=z_codes[:, cols].bitcast(FP8X4), scales=z_scales[:, cols], in_=z_woven[:])
+            for t in range(PACK):
+                product(h_banks[t], dk_q, t, (z_codes, z_scales), cols)
+                nc.scalar.activation(out=h_rows[t][:, cols], in_=h_banks[t][:, cols], func=ACT.Copy, scale=0.0625)
+
+        out_rows = out.rearrange("(p t) c -> t p c", t=PACK)
+        for t in range(PACK):
+            pa = sb.tile([P, W], F32, name=f"pa{t}")
+            pb = sb.tile([P, W], F32, name=f"pb{t}")
+            ra = sb.tile([P, W], F32, name=f"ra{t}")
+            if t == 0:
+                nc.vector.tensor_copy(pa[:], h_rows[t][:].indirect(n3_l[:]))
+            else:
+                nc.scalar.activation(out=pa[:], in_=h_rows[t][:].indirect(n3_l[:]), func=ACT.Copy)
+            nc.scalar.activation(out=pb[:], in_=h_rows[t][:].indirect(n4_l[:]), func=ACT.Copy)
+            nc.vector.tensor_tensor(ra[:], pa[:], pb[:], ALU.max)
+            nc.vector.tensor_copy(h_rows[t][:].indirect(n3_l[:]), ra[:])
+            nc.sync.dma_start(out_rows[t], h_rows[t][:])

@@ -17,7 +17,7 @@ FP8X4 = mybir.dt.float8_e4m3fn_x4
 ACT = mybir.ActivationFunctionType
 ALU = mybir.AluOpType
 
-CHUNKS = ((0, 256), (256, 128), (384, 128))
+CHUNKS = ((0, 256), (256, 256))
 W_PIECES = 2
 
 
@@ -38,28 +38,25 @@ def tile_picked_twqjointbfill_none_p_kernel(
         def entries(tile, start, count):
             return tile[:, start // 16 : (start + count) // 16]
 
-        def load_weight(name, src):
-            pieces = []
+        def load_weight(name, src, a):
             width = H // W_PIECES
-            rows = src.rearrange("(p j) c -> p j c", j=PACK)
-            for a in range(W_PIECES):
-                raw = sb.tile([P, PACK, width], F32, name=f"{name}_raw{a}")
-                nc.sync.dma_start(raw[:], rows[:, :, a * width : (a + 1) * width])
-                pieces.append(raw)
-            return pieces
+            raw = sb.tile([P, PACK, width], F32, name=f"{name}_raw{a}")
+            nc.sync.dma_start(raw[:], src.rearrange("(p j) c -> p j c", j=PACK)[:, :, a * width : (a + 1) * width])
+            return raw
 
-        def quantise_weight(name, pieces):
-            grouped = sb.tile([P, PACK * H], BF16, name=f"{name}_bf", align_bytes=64)
+        def quantise_weight(name, pieces, rounders, calls):
+            grouped = sb.tile([P, PACK * H], BF16, name=f"{name}_bf", tag=f"{name}_bf", align_bytes=64)
             codes = sb.tile([P, H], U32, name=f"{name}_codes", align_bytes=64)
             scales = sb.tile([P, H], U8, name=f"{name}_scales", align_bytes=64)
             dealt = grouped[:].rearrange("p (t m j) -> p m j t", t=PACK, j=PACK)
             per = P // len(pieces)
             for a, raw in enumerate(pieces):
-                nc.scalar.copy(out=dealt[:, a * per : (a + 1) * per], in_=raw[:].rearrange("p j (m t) -> p m j t", t=PACK))
-            for t in range(PACK):
-                cols = slice(t * P, (t + 1) * P)
+                rounders[a](out=dealt[:, a * per : (a + 1) * per], in_=raw[:].rearrange("p j (m t) -> p m j t", t=PACK))
+            width = H // calls
+            for a in range(calls):
+                cols = slice(a * width, (a + 1) * width)
                 nc.vector.quantize_mx(
-                    out=codes[:, cols].bitcast(FP8X4), scales=scales[:, cols], in_=grouped[:, t * PACK * P : (t + 1) * PACK * P]
+                    out=codes[:, cols].bitcast(FP8X4), scales=scales[:, cols], in_=grouped[:, a * PACK * width : (a + 1) * PACK * width]
                 )
             return codes, scales
 
@@ -69,30 +66,31 @@ def tile_picked_twqjointbfill_none_p_kernel(
         ds = sb.tile([P, G], U8, name="ds", align_bytes=64)
         gain = sb.tile([P, PACK], F32, name="gain")
 
-        nc.gpsimd.memset(xs[:].bitcast(I32), 0)
-        nc.gpsimd.memset(ds[:].bitcast(I32), 0)
+        nc.vector.memset(xs[:].bitcast(I32), 0)
+        nc.vector.memset(ds[:].bitcast(I32), 0)
         nc.sync.dma_start(xw[:], x_words[0].rearrange("p n t -> p (n t)").bitcast(I32))
         two_l = load_list("two_l", two)
         xs_rows = x_scales[0].bitcast(I32)
         for j in range(4):
             nc.sync.dma_start(xs[:].bitcast(I32)[j:P:32, :], xs_rows[j:16:4, :])
-        w2_raw = load_weight("w2", w2)
+        w2_raw = [load_weight("w2", w2, a) for a in range(W_PIECES)]
         offs_l = load_list("offs_l", offs)
-        w1_raw = load_weight("w1", w1)
+        w1_raw = [load_weight("w1", w1, 0)]
         n2_l = load_list("n2_l", n2)
         n1_l = load_list("n1_l", n1)
+        w1_raw.append(load_weight("w1", w1, 1))
         k1_l = load_list("k1_l", k1)
         nc.sync.dma_start(dw[:], d_words[0].rearrange("p n t -> p (n t)").bitcast(I32))
         n3_l = load_list("n3_l", n3)
         n4_l = load_list("n4_l", n4)
         ds_rows = d_scales[0].bitcast(I32)
+        nc.gpsimd.dma_start(gain[:], gs.rearrange("(p t) o -> p (t o)", t=PACK))
         for e in range(2):
             nc.gpsimd.dma_start(ds[:].bitcast(I32)[e:P:16, :], ds_rows[e:16:2, :])
-        nc.gpsimd.dma_start(gain[:], gs.rearrange("(p t) o -> p (t o)", t=PACK))
 
-        def pick(name, words, scales, offsets):
+        def pick(name, words, scales, offsets, plane_tag=""):
             codes = sb.tile([P, S], U32, name=f"{name}_codes", align_bytes=64)
-            plane = sb.tile([P, S], U8, name=f"{name}_plane", align_bytes=64)
+            plane = sb.tile([P, S], U8, name=f"{name}_plane", tag=plane_tag, align_bytes=64)
             nc.vector.tensor_copy(codes[:], words[:].bitcast(U32).indirect(offsets[:]))
             nc.vector.tensor_copy(plane[:], scales[:].indirect(offsets[:]))
             return codes, plane
@@ -111,39 +109,44 @@ def tile_picked_twqjointbfill_none_p_kernel(
 
         everything = slice(0, S)
         x_two = pick("x_two", xw, xs, two_l)
-        w2_q = quantise_weight("w2", w2_raw)
-        d_rows = []
+        w2_q = quantise_weight("w2", w2_raw, (nc.scalar.copy, nc.scalar.copy), 4)
+        d_banks = [psum.tile([P, S], F32, name=f"d_bank{t}", tag=f"dh{t}") for t in range(PACK)]
+        d_rows = [sb.tile([P, S], F32, name=f"d_row{t}") for t in range(PACK)]
         for t in range(PACK):
-            bank = psum.tile([P, S], F32, name=f"d_bank{t}", tag=f"dh{t}")
-            product(bank, w2_q, t, x_two, everything)
-            row = sb.tile([P, S], F32, name=f"d_row{t}")
-            nc.scalar.copy(out=row[:], in_=bank[:])
-            d_rows.append(row)
+            product(d_banks[t], w2_q, t, x_two, everything)
 
-        x_idx = pick("x_idx", xw, xs, offs_l)
-        w1_q = quantise_weight("w1", w1_raw)
+        x_idx = pick("x_idx", xw, xs, offs_l, plane_tag="w2_bf")
+        w1_q = quantise_weight("w1", w1_raw, (nc.scalar.copy, nc.vector.tensor_copy), 1)
         y_banks = []
         for t in range(PACK):
             bank = psum.tile([P, S], F32, name=f"y_bank{t}", tag=f"y{t}")
             product(bank, w1_q, t, x_idx, everything)
             y_banks.append(bank)
 
+        for t in range(PACK):
+            nc.scalar.copy(out=d_rows[t][:], in_=d_banks[t][:])
+
         def dictionary():
-            codes, plane = pick("d_k1", dw, ds, k1_l)
+            codes = sb.tile([P, H], U32, name="dk_picked_codes", align_bytes=64)
+            plane = sb.tile([P, H], U8, name="dk_picked_plane", align_bytes=64)
             codes_dealt = sb.tile([P, H], U32, name="dk_codes", align_bytes=64)
             plane_dealt = sb.tile([P, H], U8, name="dk_plane", align_bytes=64)
-            nc.vector.tensor_copy(plane_dealt[:].rearrange("p (t m) -> p m t", t=PACK), plane[:].rearrange("p (m t) -> p m t", t=PACK))
+            nc.vector.tensor_copy(plane[:], ds[:].indirect(k1_l[:]))
             rows = plane_dealt[:].bitcast(I32)
+            nc.vector.tensor_copy(rows.rearrange("p (t u) -> p u t", t=PACK), plane[:].bitcast(I32).rearrange("p (u t) -> p u t", t=PACK))
             for e in range(2):
                 nc.sync.dma_start(rows[2 + e : P : 32, :], rows[16 + e : P : 32, :])
-            nc.vector.tensor_copy(codes_dealt[:].rearrange("p (t m) -> p m t", t=PACK), codes[:].rearrange("p (m t) -> p m t", t=PACK))
+            nc.vector.tensor_copy(codes[:], dw[:].bitcast(U32).indirect(k1_l[:]))
+            nc.vector.tensor_copy(
+                codes_dealt[:].rearrange("p (t u b) -> p u t b", t=PACK, b=4), codes[:].rearrange("p (u t b) -> p u t b", t=PACK, b=4)
+            )
             return codes_dealt, plane_dealt
 
         z_codes = sb.tile([P, S], U32, name="z_codes", align_bytes=64)
         z_scales = sb.tile([P, S], U8, name="z_scales", align_bytes=64)
         h_banks = [psum.tile([P, S], F32, name=f"h_bank{t}", tag=f"dh{t}") for t in range(PACK)]
         h_rows = [sb.tile([P, S], F32, name=f"h_row{t}") for t in range(PACK)]
-        dk_q = None
+        dk_q = dictionary()
         for c, (start, width) in enumerate(CHUNKS):
             cols = slice(start, start + width)
             z_planes = sb.tile([P, PACK, width], BF16, name=f"z_planes{c}")
@@ -152,27 +155,33 @@ def tile_picked_twqjointbfill_none_p_kernel(
                 diff = sb.tile([P, width], F32, name=f"diff{c}_{t}")
                 bent = sb.tile([P, width], F32, name=f"bent{c}_{t}")
                 nc.scalar.activation(out=second[:], in_=d_rows[t][:].indirect(entries(n2_l, start, width)), func=ACT.Copy)
-                nc.vector.tensor_tensor(diff[:], d_rows[t][:].indirect(entries(n1_l, start, width)), second[:], ALU.subtract)
+                if c >= 1 and t == 3:
+                    first = sb.tile([P, width], F32, name=f"first{c}_{t}")
+                    nc.scalar.activation(out=first[:], in_=d_rows[t][:].indirect(entries(n1_l, start, width)), func=ACT.Copy)
+                    nc.vector.tensor_tensor(diff[:], first[:], second[:], ALU.subtract)
+                else:
+                    nc.vector.tensor_tensor(diff[:], d_rows[t][:].indirect(entries(n1_l, start, width)), second[:], ALU.subtract)
                 nc.scalar.activation(out=bent[:], in_=diff[:], func=ACT.Tanh)
                 nc.vector.scalar_tensor_tensor(
                     out=z_planes[:, t, :], in0=y_banks[t][:, cols], scalar=gain[:, t : t + 1], in1=bent[:], op0=ALU.mult, op1=ALU.mult
                 )
-            if c == 0:
-                dk_q = dictionary()
             z_woven = sb.tile([P, PACK * width], BF16, name=f"z_woven{c}", align_bytes=64)
-            nc.vector.tensor_copy(
+            weave = nc.scalar.copy if c == 0 else nc.vector.tensor_copy
+            weave(
                 z_woven[:].rearrange("p (c i t) -> p c t i", i=4, t=PACK), z_planes[:].rearrange("p t (c i) -> p c t i", i=4)
             )
             nc.vector.quantize_mx(out=z_codes[:, cols].bitcast(FP8X4), scales=z_scales[:, cols], in_=z_woven[:])
             for t in range(PACK):
                 product(h_banks[t], dk_q, t, (z_codes, z_scales), cols)
-                nc.scalar.activation(out=h_rows[t][:, cols], in_=h_banks[t][:, cols], func=ACT.Copy, scale=0.0625)
+                if c + 1 < len(CHUNKS):
+                    nc.scalar.activation(out=h_rows[t][:, cols], in_=h_banks[t][:, cols], func=ACT.Copy, scale=0.0625)
 
-        out_rows = out.rearrange("(p t) c -> t p c", t=PACK)
+        out_rows = out.rearrange("(u t b) c -> t u b c", t=PACK, b=4)
         for t in range(PACK):
             pa = sb.tile([P, W], F32, name=f"pa{t}")
             pb = sb.tile([P, W], F32, name=f"pb{t}")
             ra = sb.tile([P, W], F32, name=f"ra{t}")
+            nc.scalar.activation(out=h_rows[t][:, cols], in_=h_banks[t][:, cols], func=ACT.Copy, scale=0.0625)
             if t == 0:
                 nc.vector.tensor_copy(pa[:], h_rows[t][:].indirect(n3_l[:]))
             else:

@@ -17,7 +17,7 @@ FP8X4 = mybir.dt.float8_e4m3fn_x4
 ACT = mybir.ActivationFunctionType
 ALU = mybir.AluOpType
 
-CHUNKS = ((0, 256), (256, 256))
+CHUNKS = ((0, 256), (256, 128), (384, 128))
 W_PIECES = 2
 
 
@@ -50,8 +50,9 @@ def tile_picked_twqjointbfill_none_p_kernel(
             scales = sb.tile([P, H], U8, name=f"{name}_scales", align_bytes=64)
             dealt = grouped[:].rearrange("p (t m j) -> p m j t", t=PACK, j=PACK)
             per = P // len(pieces)
-            for a, raw in enumerate(pieces):
-                rounders[a](out=dealt[:, a * per : (a + 1) * per], in_=raw[:].rearrange("p j (m t) -> p m j t", t=PACK))
+            for copy, m0, m1 in rounders:
+                raw = pieces[m0 // per][:].rearrange("p j (m t) -> p m j t", t=PACK)
+                copy(out=dealt[:, m0:m1], in_=raw[:, m0 % per : m0 % per + m1 - m0])
             width = H // calls
             for a in range(calls):
                 cols = slice(a * width, (a + 1) * width)
@@ -109,14 +110,14 @@ def tile_picked_twqjointbfill_none_p_kernel(
 
         everything = slice(0, S)
         x_two = pick("x_two", xw, xs, two_l)
-        w2_q = quantise_weight("w2", w2_raw, (nc.scalar.copy, nc.scalar.copy), 4)
+        w2_q = quantise_weight("w2", w2_raw, ((nc.scalar.copy, 0, 64), (nc.scalar.copy, 64, 96), (nc.vector.tensor_copy, 96, 128)), 4)
         d_banks = [psum.tile([P, S], F32, name=f"d_bank{t}", tag=f"dh{t}") for t in range(PACK)]
         d_rows = [sb.tile([P, S], F32, name=f"d_row{t}") for t in range(PACK)]
         for t in range(PACK):
             product(d_banks[t], w2_q, t, x_two, everything)
 
-        x_idx = pick("x_idx", xw, xs, offs_l, plane_tag="w2_bf")
-        w1_q = quantise_weight("w1", w1_raw, (nc.scalar.copy, nc.vector.tensor_copy), 1)
+        x_idx = pick("x_idx", xw, xs, offs_l)
+        w1_q = quantise_weight("w1", w1_raw, ((nc.scalar.copy, 0, 64), (nc.vector.tensor_copy, 64, 128)), 1)
         y_banks = []
         for t in range(PACK):
             bank = psum.tile([P, S], F32, name=f"y_bank{t}", tag=f"y{t}")
@@ -155,7 +156,7 @@ def tile_picked_twqjointbfill_none_p_kernel(
                 diff = sb.tile([P, width], F32, name=f"diff{c}_{t}")
                 bent = sb.tile([P, width], F32, name=f"bent{c}_{t}")
                 nc.scalar.activation(out=second[:], in_=d_rows[t][:].indirect(entries(n2_l, start, width)), func=ACT.Copy)
-                if c >= 1 and t == 3:
+                if t == 3:
                     first = sb.tile([P, width], F32, name=f"first{c}_{t}")
                     nc.scalar.activation(out=first[:], in_=d_rows[t][:].indirect(entries(n1_l, start, width)), func=ACT.Copy)
                     nc.vector.tensor_tensor(diff[:], first[:], second[:], ALU.subtract)
@@ -189,4 +190,8 @@ def tile_picked_twqjointbfill_none_p_kernel(
             nc.scalar.activation(out=pb[:], in_=h_rows[t][:].indirect(n4_l[:]), func=ACT.Copy)
             nc.vector.tensor_tensor(ra[:], pa[:], pb[:], ALU.max)
             nc.vector.tensor_copy(h_rows[t][:].indirect(n3_l[:]), ra[:])
-            nc.sync.dma_start(out_rows[t], h_rows[t][:])
+            if t + 1 < PACK:
+                nc.sync.dma_start(out_rows[t], h_rows[t][:])
+            else:
+                nc.sync.dma_start(out_rows[t][:, :, : S // 2], h_rows[t][:, : S // 2])
+                nc.scalar.dma_start(out_rows[t][:, :, S // 2 :], h_rows[t][:, S // 2 :])

@@ -17,7 +17,7 @@ FP8X4 = mybir.dt.float8_e4m3fn_x4
 ACT = mybir.ActivationFunctionType
 ALU = mybir.AluOpType
 
-CHUNKS = ((0, 256), (256, 128), (384, 128))
+CHUNKS = ((0, 256), (256, 256))
 W_PIECES = 2
 
 
@@ -110,13 +110,13 @@ def tile_picked_twqjointbfill_none_p_kernel(
 
         everything = slice(0, S)
         x_two = pick("x_two", xw, xs, two_l)
-        w2_q = quantise_weight("w2", w2_raw, ((nc.scalar.copy, 0, 64), (nc.scalar.copy, 64, 96), (nc.vector.tensor_copy, 96, 128)), 4)
+        w2_q = quantise_weight("w2", w2_raw, ((nc.scalar.copy, 0, 64), (nc.scalar.copy, 64, 128)), 4)
         d_banks = [psum.tile([P, S], F32, name=f"d_bank{t}", tag=f"dh{t}") for t in range(PACK)]
         d_rows = [sb.tile([P, S], F32, name=f"d_row{t}") for t in range(PACK)]
         for t in range(PACK):
             product(d_banks[t], w2_q, t, x_two, everything)
 
-        x_idx = pick("x_idx", xw, xs, offs_l)
+        x_idx = pick("x_idx", xw, xs, offs_l, plane_tag="w2_bf")
         w1_q = quantise_weight("w1", w1_raw, ((nc.scalar.copy, 0, 64), (nc.vector.tensor_copy, 64, 128)), 1)
         y_banks = []
         for t in range(PACK):
@@ -156,7 +156,7 @@ def tile_picked_twqjointbfill_none_p_kernel(
                 diff = sb.tile([P, width], F32, name=f"diff{c}_{t}")
                 bent = sb.tile([P, width], F32, name=f"bent{c}_{t}")
                 nc.scalar.activation(out=second[:], in_=d_rows[t][:].indirect(entries(n2_l, start, width)), func=ACT.Copy)
-                if t == 3:
+                if c >= 1 and t == 3:
                     first = sb.tile([P, width], F32, name=f"first{c}_{t}")
                     nc.scalar.activation(out=first[:], in_=d_rows[t][:].indirect(entries(n1_l, start, width)), func=ACT.Copy)
                     nc.vector.tensor_tensor(diff[:], first[:], second[:], ALU.subtract)
@@ -168,30 +168,37 @@ def tile_picked_twqjointbfill_none_p_kernel(
                 )
             z_woven = sb.tile([P, PACK * width], BF16, name=f"z_woven{c}", align_bytes=64)
             weave = nc.scalar.copy if c == 0 else nc.vector.tensor_copy
-            weave(
-                z_woven[:].rearrange("p (c i t) -> p c t i", i=4, t=PACK), z_planes[:].rearrange("p t (c i) -> p c t i", i=4)
-            )
-            nc.vector.quantize_mx(out=z_codes[:, cols].bitcast(FP8X4), scales=z_scales[:, cols], in_=z_woven[:])
+            step = width if c == 0 else width // 2
+            for s0 in range(0, width, step):
+                weave(
+                    z_woven[:, PACK * s0 : PACK * (s0 + step)].rearrange("p (c i t) -> p c t i", i=4, t=PACK),
+                    z_planes[:, :, s0 : s0 + step].rearrange("p t (c i) -> p c t i", i=4),
+                )
+            for s0 in range(0, width, step):
+                part = slice(start + s0, start + s0 + step)
+                nc.vector.quantize_mx(
+                    out=z_codes[:, part].bitcast(FP8X4), scales=z_scales[:, part], in_=z_woven[:, PACK * s0 : PACK * (s0 + step)]
+                )
             for t in range(PACK):
-                product(h_banks[t], dk_q, t, (z_codes, z_scales), cols)
+                for s0 in range(0, width, step if t == 0 else width):
+                    part = slice(start + s0, start + s0 + (step if t == 0 else width))
+                    product(h_banks[t], dk_q, t, (z_codes, z_scales), part)
                 if c + 1 < len(CHUNKS):
                     nc.scalar.activation(out=h_rows[t][:, cols], in_=h_banks[t][:, cols], func=ACT.Copy, scale=0.0625)
 
         out_rows = out.rearrange("(u t b) c -> t u b c", t=PACK, b=4)
-        for t in range(PACK):
-            pa = sb.tile([P, W], F32, name=f"pa{t}")
-            pb = sb.tile([P, W], F32, name=f"pb{t}")
-            ra = sb.tile([P, W], F32, name=f"ra{t}")
-            nc.scalar.activation(out=h_rows[t][:, cols], in_=h_banks[t][:, cols], func=ACT.Copy, scale=0.0625)
-            if t == 0:
-                nc.vector.tensor_copy(pa[:], h_rows[t][:].indirect(n3_l[:]))
-            else:
-                nc.scalar.activation(out=pa[:], in_=h_rows[t][:].indirect(n3_l[:]), func=ACT.Copy)
-            nc.scalar.activation(out=pb[:], in_=h_rows[t][:].indirect(n4_l[:]), func=ACT.Copy)
+        for group in ((0,), (1,), (2, 3)):
+            pa = sb.tile([P, len(group), W], F32, name=f"pa{group[0]}")
+            pb = sb.tile([P, len(group), W], F32, name=f"pb{group[0]}")
+            ra = sb.tile([P, len(group), W], F32, name=f"ra{group[0]}")
+            for g, t in enumerate(group):
+                nc.scalar.activation(out=h_rows[t][:, cols], in_=h_banks[t][:, cols], func=ACT.Copy, scale=0.0625)
+                if t == 0:
+                    nc.vector.tensor_copy(pa[:, g, :], h_rows[t][:].indirect(n3_l[:]))
+                else:
+                    nc.scalar.activation(out=pa[:, g, :], in_=h_rows[t][:].indirect(n3_l[:]), func=ACT.Copy)
+                nc.scalar.activation(out=pb[:, g, :], in_=h_rows[t][:].indirect(n4_l[:]), func=ACT.Copy)
             nc.vector.tensor_tensor(ra[:], pa[:], pb[:], ALU.max)
-            nc.vector.tensor_copy(h_rows[t][:].indirect(n3_l[:]), ra[:])
-            if t + 1 < PACK:
+            for g, t in enumerate(group):
+                nc.vector.tensor_copy(h_rows[t][:].indirect(n3_l[:]), ra[:, g, :])
                 nc.sync.dma_start(out_rows[t], h_rows[t][:])
-            else:
-                nc.sync.dma_start(out_rows[t][:, :, : S // 2], h_rows[t][:, : S // 2])
-                nc.scalar.dma_start(out_rows[t][:, :, S // 2 :], h_rows[t][:, S // 2 :])

from contextlib import ExitStack

import concourse.mybir as mybir

K, T, S, H, G, W = 512, 1024, 512, 512, 2048, 256
P = 128
PACK = 4
FLOPS = 3 * 2 * K * H * S

F32 = mybir.dt.float32
BF16 = mybir.dt.bfloat16
I32 = mybir.dt.int32
U32 = mybir.dt.uint32
U16 = mybir.dt.uint16
U8 = mybir.dt.uint8
FP8X4 = mybir.dt.float8_e4m3fn_x4
ACT = mybir.ActivationFunctionType
ALU = mybir.AluOpType

CHUNKS = ((0, 256), (256, 256))
W_PIECES = 2


def tile_picked_twqjointbfill_none_p_kernel(
    tc, x_words, x_scales, w1, w2, gs, d_words, d_scales, offs, two, n1, n2, k1, n3, n4, out
):
    nc = tc.nc
    with ExitStack() as ctx:
        lists = ctx.enter_context(tc.tile_pool(name="lists", bufs=1))
        sb = ctx.enter_context(tc.tile_pool(name="sb", bufs=1))
        psum = ctx.enter_context(tc.psum_pool(name="psum", bufs=1))

        def load_list(name, src):
            tile = lists.tile([P, src.shape[1]], U16, name=name)
            nc.sync.dma_start(tile[:], src)
            return tile

        def entries(tile, start, count):
            return tile[:, start // 16 : (start + count) // 16]

        def load_weight(name, src, a):
            width = H // W_PIECES
            raw = sb.tile([P, PACK, width], F32, name=f"{name}_raw{a}")
            nc.sync.dma_start(raw[:], src.rearrange("(p j) c -> p j c", j=PACK)[:, :, a * width : (a + 1) * width])
            return raw

        def quantise_weight(name, pieces, rounders, calls):
            grouped = sb.tile([P, PACK * H], BF16, name=f"{name}_bf", tag=f"{name}_bf", align_bytes=64)
            codes = sb.tile([P, H], U32, name=f"{name}_codes", align_bytes=64)
            scales = sb.tile([P, H], U8, name=f"{name}_scales", align_bytes=64)
            dealt = grouped[:].rearrange("p (t m j) -> p m j t", t=PACK, j=PACK)
            per = P // len(pieces)
            for copy, m0, m1 in rounders:
                raw = pieces[m0 // per][:].rearrange("p j (m t) -> p m j t", t=PACK)
                copy(out=dealt[:, m0:m1], in_=raw[:, m0 % per : m0 % per + m1 - m0])
            width = H // calls
            for a in range(calls):
                cols = slice(a * width, (a + 1) * width)
                nc.vector.quantize_mx(
                    out=codes[:, cols].bitcast(FP8X4), scales=scales[:, cols], in_=grouped[:, a * PACK * width : (a + 1) * PACK * width]
                )
            return codes, scales

        xw = sb.tile([P, T], I32, name="xw", align_bytes=64)
        xs = sb.tile([P, T], U8, name="xs", align_bytes=64)
        dw = sb.tile([P, G], I32, name="dw", align_bytes=64)
        ds = sb.tile([P, G], U8, name="ds", align_bytes=64)
        gain = sb.tile([P, PACK], F32, name="gain")

        nc.vector.memset(xs[:].bitcast(I32), 0)
        nc.vector.memset(ds[:].bitcast(I32), 0)
        nc.sync.dma_start(xw[:], x_words[0].rearrange("p n t -> p (n t)").bitcast(I32))
        two_l = load_list("two_l", two)
        xs_rows = x_scales[0].bitcast(I32)
        for j in range(4):
            nc.sync.dma_start(xs[:].bitcast(I32)[j:P:32, :], xs_rows[j:16:4, :])
        w2_raw = [load_weight("w2", w2, a) for a in range(W_PIECES)]
        offs_l = load_list("offs_l", offs)
        w1_raw = [load_weight("w1", w1, 0)]
        n2_l = load_list("n2_l", n2)
        n1_l = load_list("n1_l", n1)
        w1_raw.append(load_weight("w1", w1, 1))
        k1_l = load_list("k1_l", k1)
        nc.sync.dma_start(dw[:], d_words[0].rearrange("p n t -> p (n t)").bitcast(I32))
        n3_l = load_list("n3_l", n3)
        n4_l = load_list("n4_l", n4)
        ds_rows = d_scales[0].bitcast(I32)
        nc.gpsimd.dma_start(gain[:], gs.rearrange("(p t) o -> p (t o)", t=PACK))
        for e in range(2):
            nc.gpsimd.dma_start(ds[:].bitcast(I32)[e:P:16, :], ds_rows[e:16:2, :])

        def pick(name, words, scales, offsets, plane_tag=""):
            codes = sb.tile([P, S], U32, name=f"{name}_codes", align_bytes=64)
            plane = sb.tile([P, S], U8, name=f"{name}_plane", tag=plane_tag, align_bytes=64)
            nc.vector.tensor_copy(codes[:], words[:].bitcast(U32).indirect(offsets[:]))
            nc.vector.tensor_copy(plane[:], scales[:].indirect(offsets[:]))
            return codes, plane

        def product(bank, stat, t, mov, cols):
            tcols = slice(t * P, (t + 1) * P)
            nc.tensor.matmul_mx(
                out=bank[:, cols],
                lhsT=stat[0][:, tcols].bitcast(FP8X4),
                lhsT_scale=stat[1][:, tcols],
                rhs=mov[0][:, cols].bitcast(FP8X4),
                rhs_scale=mov[1][:, cols],
                start=True,
                stop=True,
            )

        everything = slice(0, S)
        x_two = pick("x_two", xw, xs, two_l)
        w2_q = quantise_weight("w2", w2_raw, ((nc.scalar.copy, 0, 64), (nc.scalar.copy, 64, 128)), 4)
        d_banks = [psum.tile([P, S], F32, name=f"d_bank{t}", tag=f"dh{t}") for t in range(PACK)]
        d_rows = [sb.tile([P, S], F32, name=f"d_row{t}") for t in range(PACK)]
        for t in range(PACK):
            product(d_banks[t], w2_q, t, x_two, everything)

        x_idx = pick("x_idx", xw, xs, offs_l, plane_tag="w2_bf")
        w1_q = quantise_weight("w1", w1_raw, ((nc.scalar.copy, 0, 64), (nc.vector.tensor_copy, 64, 128)), 1)
        y_banks = []
        for t in range(PACK):
            bank = psum.tile([P, S], F32, name=f"y_bank{t}", tag=f"y{t}")
            product(bank, w1_q, t, x_idx, everything)
            y_banks.append(bank)

        for t in range(PACK):
            nc.scalar.copy(out=d_rows[t][:], in_=d_banks[t][:])

        def dictionary():
            codes = sb.tile([P, H], U32, name="dk_picked_codes", align_bytes=64)
            plane = sb.tile([P, H], U8, name="dk_picked_plane", align_bytes=64)
            codes_dealt = sb.tile([P, H], U32, name="dk_codes", align_bytes=64)
            plane_dealt = sb.tile([P, H], U8, name="dk_plane", align_bytes=64)
            nc.vector.tensor_copy(plane[:], ds[:].indirect(k1_l[:]))
            rows = plane_dealt[:].bitcast(I32)
            nc.vector.tensor_copy(rows.rearrange("p (t u) -> p u t", t=PACK), plane[:].bitcast(I32).rearrange("p (u t) -> p u t", t=PACK))
            for e in range(2):
                nc.sync.dma_start(rows[2 + e : P : 32, :], rows[16 + e : P : 32, :])
            nc.vector.tensor_copy(codes[:], dw[:].bitcast(U32).indirect(k1_l[:]))
            nc.vector.tensor_copy(
                codes_dealt[:].rearrange("p (t u b) -> p u t b", t=PACK, b=4), codes[:].rearrange("p (u t b) -> p u t b", t=PACK, b=4)
            )
            return codes_dealt, plane_dealt

        z_codes = sb.tile([P, S], U32, name="z_codes", align_bytes=64)
        z_scales = sb.tile([P, S], U8, name="z_scales", align_bytes=64)
        h_banks = [psum.tile([P, S], F32, name=f"h_bank{t}", tag=f"dh{t}") for t in range(PACK)]
        h_rows = [sb.tile([P, S], F32, name=f"h_row{t}") for t in range(PACK)]
        dk_q = dictionary()
        for c, (start, width) in enumerate(CHUNKS):
            cols = slice(start, start + width)
            z_planes = sb.tile([P, PACK, width], BF16, name=f"z_planes{c}")
            for t in range(PACK):
                second = sb.tile([P, width], F32, name=f"second{c}_{t}")
                diff = sb.tile([P, width], F32, name=f"diff{c}_{t}")
                bent = sb.tile([P, width], F32, name=f"bent{c}_{t}")
                nc.scalar.activation(out=second[:], in_=d_rows[t][:].indirect(entries(n2_l, start, width)), func=ACT.Copy)
                if c >= 1 and t == 3:
                    first = sb.tile([P, width], F32, name=f"first{c}_{t}")
                    nc.scalar.activation(out=first[:], in_=d_rows[t][:].indirect(entries(n1_l, start, width)), func=ACT.Copy)
                    nc.vector.tensor_tensor(diff[:], first[:], second[:], ALU.subtract)
                else:
                    nc.vector.tensor_tensor(diff[:], d_rows[t][:].indirect(entries(n1_l, start, width)), second[:], ALU.subtract)
                nc.scalar.activation(out=bent[:], in_=diff[:], func=ACT.Tanh)
                nc.vector.scalar_tensor_tensor(
                    out=z_planes[:, t, :], in0=y_banks[t][:, cols], scalar=gain[:, t : t + 1], in1=bent[:], op0=ALU.mult, op1=ALU.mult
                )
            z_woven = sb.tile([P, PACK * width], BF16, name=f"z_woven{c}", align_bytes=64)
            weave = nc.scalar.copy if c == 0 else nc.vector.tensor_copy
            step = width if c == 0 else width // 2
            for s0 in range(0, width, step):
                weave(
                    z_woven[:, PACK * s0 : PACK * (s0 + step)].rearrange("p (c i t) -> p c t i", i=4, t=PACK),
                    z_planes[:, :, s0 : s0 + step].rearrange("p t (c i) -> p c t i", i=4),
                )
            for s0 in range(0, width, step):
                part = slice(start + s0, start + s0 + step)
                nc.vector.quantize_mx(
                    out=z_codes[:, part].bitcast(FP8X4), scales=z_scales[:, part], in_=z_woven[:, PACK * s0 : PACK * (s0 + step)]
                )
            for t in range(PACK):
                for s0 in range(0, width, step if t == 0 else width):
                    part = slice(start + s0, start + s0 + (step if t == 0 else width))
                    product(h_banks[t], dk_q, t, (z_codes, z_scales), part)
                if c + 1 < len(CHUNKS):
                    nc.scalar.activation(out=h_rows[t][:, cols], in_=h_banks[t][:, cols], func=ACT.Copy, scale=0.0625)

        out_rows = out.rearrange("(u t b) c -> t u b c", t=PACK, b=4)
        for group in ((0,), (1,), (2, 3)):
            pa = sb.tile([P, len(group), W], F32, name=f"pa{group[0]}")
            pb = sb.tile([P, len(group), W], F32, name=f"pb{group[0]}")
            ra = sb.tile([P, len(group), W], F32, name=f"ra{group[0]}")
            for g, t in enumerate(group):
                nc.scalar.activation(out=h_rows[t][:, cols], in_=h_banks[t][:, cols], func=ACT.Copy, scale=0.0625)
                if t == 0:
                    nc.vector.tensor_copy(pa[:, g, :], h_rows[t][:].indirect(n3_l[:]))
                else:
                    nc.scalar.activation(out=pa[:, g, :], in_=h_rows[t][:].indirect(n3_l[:]), func=ACT.Copy)
                nc.scalar.activation(out=pb[:, g, :], in_=h_rows[t][:].indirect(n4_l[:]), func=ACT.Copy)
            nc.vector.tensor_tensor(ra[:], pa[:], pb[:], ALU.max)
            for g, t in enumerate(group):
                nc.vector.tensor_copy(h_rows[t][:].indirect(n3_l[:]), ra[:, g, :])
                nc.sync.dma_start(out_rows[t], h_rows[t][:])
